import numpy as np
import ml_dtypes


def mxq(x, axis, fmt="e4m3"):
    dtype, down = {"e4m3": (ml_dtypes.float8_e4m3fn, 7), "e5m2": (ml_dtypes.float8_e5m2, 14)}[fmt]
    v = np.moveaxis(np.asarray(x, np.float32).astype(ml_dtypes.bfloat16).astype(np.float64), axis, -1)
    blocks = v.reshape(v.shape[:-1] + (-1, 32))
    amax = np.abs(blocks).max(-1, keepdims=True)
    byte = np.maximum(np.where(amax > 0, np.frexp(amax)[1] - 1 + 127, 0) - down, 1)
    scale = np.exp2(byte - 127.0)
    codes = (blocks / scale).astype(np.float32).astype(dtype).astype(np.float64)
    return np.moveaxis((codes * scale).reshape(v.shape), -1, axis)


WIDE = False


def mx_kscale(k, group=512):
    if not WIDE:
        return np.ones(k)
    levels = np.array([18, -18])
    if group != 512:
        return np.exp2(np.random.permutation(np.resize(levels, k // group))).repeat(group)
    if k % 512:
        return np.exp2(np.random.permutation(np.resize(levels, k // 32))).repeat(32)
    a = np.empty((k // 512, 16))
    for p in range(k // 512):
        a[p, :8] = np.random.permutation(np.resize(levels, 8))
        for g in range(8):
            far = levels[np.abs(levels - a[p, g]) >= 10]
            a[p, g + 8] = far[np.random.randint(len(far))]
    return np.exp2(a.ravel()).repeat(32)


def f64(x):
    return np.asarray(x).astype(np.float64)


def silu(v):
    return v / (1.0 + np.exp(-v))


G, D, M, N = 8, 128, 128, 512


def sgn(shape):
    return np.random.uniform(0.5, 2.0, shape) * np.where(np.random.standard_normal(shape) < 0, -1.0, 1.0)


def setup_inputs():
    n = np.random.standard_normal
    s_d = mx_kscale(D, 0)
    return {
        "x": (n((D, N)) * s_d[:, None]).astype(np.float32),
        "w": (n((G, D, M)) / np.sqrt(D) / s_d[:, None]).astype(np.float32),
        "ew": (sgn((G, M, 1))).astype(np.float32),
        "u": (n((G, D, M)) / np.sqrt(D) / s_d[:, None]).astype(np.float32),
    }


def reference(x, w, ew, u):
    wq = mxq(f64(w), 1, "e4m3")
    xq = mxq(f64(x), 0, "e4m3")
    z = wq.transpose(0, 2, 1) @ xq
    uq = mxq(f64(u), 1, "e4m3")
    z2 = uq.transpose(0, 2, 1) @ xq
    y = silu(z) * z2 * f64(ew)
    s = y.sum(0)
    return s

from contextlib import ExitStack

import concourse.mybir as mybir

G, D, M, N = 8, 128, 128, 512
FLOPS = 2 * 2 * G * D * M * N

F32 = mybir.dt.float32
BF16 = mybir.dt.bfloat16
I32 = mybir.dt.int32
U8 = mybir.dt.uint8
FP8X4 = mybir.dt.float8_e4m3fn_x4
ALU = mybir.AluOpType
ACT = mybir.ActivationFunctionType

P = 128
PACK = 4
ROWS = D // PACK
TILES = P // ROWS
HALF = N // 2
PASS_N = 128
X_VECTOR_COLS = 176


def interleave(copy, grouped, raw, c0, c1):
    copy(
        out=grouped[:, c0:c1, :].rearrange("p (c i) j -> p c j i", i=4),
        in_=raw[:, :, c0:c1].rearrange("p j (c i) -> p c j i", i=4),
    )


def tile_rows_mexp_glu_kernel(tc, x, w, ew, u, out):
    nc = tc.nc
    with ExitStack() as ctx:
        sb = ctx.enter_context(tc.tile_pool(name="sb", bufs=1))
        ps = ctx.enter_context(tc.psum_pool(name="ps", bufs=1))
        ctx.enter_context(tc.manual_schedule())

        def packed(name, width):
            return sb.tile([P, width + width // 4], I32, name=name, align_bytes=64)

        def codes(t, width, q, c0, c1):
            return t[ROWS * q : ROWS * (q + 1), c0:c1].bitcast(FP8X4)

        def scales(t, width, q, c0, c1):
            return t[ROWS * q : ROWS * (q + 1), width + c0 // 4 : width + c1 // 4].bitcast(U8)

        def quantize(t, width, grouped):
            nc.vector.quantize_mx(
                out=t[:, 0:width].bitcast(FP8X4),
                scales=t[:, width : width + width // 4].bitcast(U8),
                in_=grouped[:].rearrange("p c j -> p (c j)"),
            )

        x_own = packed("x_own", HALF)
        x_other = packed("x_other", HALF)
        ew_rows = sb.tile([P, G * 32], F32, name="ew_rows", align_bytes=64)
        ew_cols = sb.tile([P, G * 32], F32, name="ew_cols", align_bytes=64)
        warm_in = sb.tile([P, 8], F32, name="warm_in")
        warm_out = sb.tile([P, 8], F32, name="warm_out")
        nc.vector.memset(ew_rows[:], 0.0)
        nc.vector.memset(warm_in[:], 0.0)
        nc.vector.memset(x_own[:, HALF:], 0)

        x_raw = sb.tile([P, PACK, HALF], F32, name="x_raw")
        x_rows = x.rearrange("(p j) n -> p j n", j=PACK)
        for q in (0, 2, 1, 3):
            h = q // 2
            queue = nc.sync if h == 0 else nc.scalar
            queue.dma_start(out=x_raw[ROWS * q : ROWS * (q + 1)], in_=x_rows[:, :, HALF * h : HALF * (h + 1)])
        nc.scalar.dma_start(
            out=ew_rows[0:P:32, :].rearrange("a (g i) -> a g i", i=32),
            in_=ew.rearrange("g (a i) o -> a g (i o)", i=32),
        )
        raw = {}
        for s in range(2):
            for name, src in (("w", w), ("u", u)):
                t = sb.tile([P, PACK, M], F32, name="raw_%s%d" % (name, s))
                nc.sync.dma_start(out=t[:], in_=src[TILES * s : TILES * (s + 1)].rearrange("g (p j) m -> (g p) j m", j=PACK))
                raw[name, s] = t
        nc.scalar.activation(out=warm_out[:], in_=warm_in[:], func=ACT.Silu)

        x_bf = sb.tile([P, HALF, PACK], BF16, name="x_bf", align_bytes=64)
        w0_bf = sb.tile([P, M, PACK], BF16, name="w0_bf", align_bytes=64)
        u0_bf = sb.tile([P, M, PACK], BF16, name="u0_bf", align_bytes=64)
        wu1_bf = sb.tile([P, 2 * M, PACK], BF16, name="wu1_bf", align_bytes=64)
        w0_q = packed("w0_q", M)
        u0_q = packed("u0_q", M)
        wu1_q = packed("wu1_q", 2 * M)
        stationary = {
            ("w", 0): (w0_q, M, 0),
            ("u", 0): (u0_q, M, 0),
            ("w", 1): (wu1_q, 2 * M, 0),
            ("u", 1): (wu1_q, 2 * M, M),
        }

        banks = [[ps.tile([P, N], F32, name="bank_%d_%d" % (q, b)) for b in range(2)] for q in range(TILES)]

        def product(dst, name, s, moving, q):
            t, width, c0 = stationary[name, s]
            for c in range(0, HALF, PASS_N):
                nc.tensor.matmul_mx(
                    out=dst[:, c : c + PASS_N],
                    lhsT=codes(t, width, q, c0, c0 + M),
                    lhsT_scale=scales(t, width, q, c0, c0 + M),
                    rhs=codes(moving, HALF, q, c, c + PASS_N),
                    rhs_scale=scales(moving, HALF, q, c, c + PASS_N),
                    start=True,
                    stop=True,
                )

        def z_of(step, q):
            if step == 0:
                return banks[q][0][:, 0:HALF], banks[q][1][:, 0:HALF]
            bank = banks[q][(step + 1) % 2]
            return bank[:, 0:HALF], bank[:, HALF:N]

        interleave(nc.vector.tensor_copy, x_bf, x_raw, 0, X_VECTOR_COLS)
        interleave(nc.scalar.copy, x_bf, x_raw, X_VECTOR_COLS, HALF)
        interleave(nc.scalar.copy, w0_bf, raw["w", 0], 0, M)
        quantize(x_own, HALF, x_bf)
        nc.sync.dma_start(out=x_other[0:64, :], in_=x_own[64:P, :])
        nc.sync.dma_start(out=x_other[64:P, :], in_=x_own[0:64, :])
        interleave(nc.vector.tensor_copy, u0_bf, raw["u", 0], 0, M)
        quantize(w0_q, M, w0_bf)
        for q in range(TILES):
            product(z_of(0, q)[0], "w", 0, x_own, q)
        quantize(u0_q, M, u0_bf)
        for q in range(TILES):
            product(z_of(0, q)[1], "u", 0, x_own, q)
        nc.vector.transpose(out=ew_cols[:], in_=ew_rows[:])
        interleave(nc.vector.tensor_copy, wu1_bf[:, 0:M, :], raw["w", 1], 0, M)
        interleave(nc.vector.tensor_copy, wu1_bf[:, M : 2 * M, :], raw["u", 1], 0, M)

        def tiles_of(step):
            return (0, 1, 2, 3) if step < 2 else (2, 3, 0, 1)

        def fill(step, q):
            z, z2 = z_of(step, q)
            moving = x_own if step < 2 else x_other
            product(z, "w", step % 2, moving, q)
            product(z2, "u", step % 2, moving, q)

        terms = {}
        pairs = {}
        for step in range(4):
            for i, q in enumerate(tiles_of(step)):
                z, z2 = z_of(step, q)
                g = TILES * (step % 2) + q
                gate = sb.tile([P, HALF], F32, name="gate_%d_%d" % (step, i))
                nc.scalar.activation(out=gate[:], in_=z, func=ACT.Silu)
                term = sb.tile([P, HALF], F32, name="term_%d_%d" % (step, i))
                nc.vector.scalar_tensor_tensor(
                    out=term[:], in0=z2, scalar=ew_cols[:, 32 * g : 32 * g + 1], in1=gate[:], op0=ALU.mult, op1=ALU.mult
                )
                terms[step, i] = term
                if step == 0 and i == 0:
                    quantize(wu1_q, 2 * M, wu1_bf)
                if step == 0:
                    fill(1, q)
                if i % 2 == 1 and step < 3:
                    pair = sb.tile([P, HALF], F32, name="pair_%d_%d" % (step, i // 2))
                    nc.gpsimd.tensor_tensor(out=pair[:], in0=terms[step, i - 1][:], in1=term[:], op=ALU.add)
                    pairs[step, i // 2] = pair
            if step < 2:
                for q in tiles_of(step + 2):
                    fill(step + 2, q)

        def add(name, a, b):
            t = sb.tile([P, HALF], F32, name=name)
            nc.vector.tensor_tensor(out=t[:], in0=a[:], in1=b[:], op=ALU.add)
            return t

        a01 = add("a01", pairs[0, 0], pairs[1, 0])
        a3 = add("a3", terms[3, 0], terms[3, 1])
        a012 = add("a012", a01, pairs[2, 0])
        b3 = add("b3", terms[3, 2], terms[3, 3])
        a_all = add("a_all", a012, a3)
        nc.sync.dma_start(out=out[:, 0:HALF], in_=a_all[:])
        b01 = add("b01", pairs[0, 1], pairs[1, 1])
        b23 = add("b23", pairs[2, 1], b3)
        b_all = add("b_all", b01, b23)
        nc.sync.dma_start(out=out[:, HALF:N], in_=b_all[:])
